import numpy as np
import ml_dtypes


def mxq(x, axis, fmt="e4m3"):
    dtype, down = {"e4m3": (ml_dtypes.float8_e4m3fn, 7), "e5m2": (ml_dtypes.float8_e5m2, 14)}[fmt]
    v = np.moveaxis(np.asarray(x, np.float32).astype(ml_dtypes.bfloat16).astype(np.float64), axis, -1)
    blocks = v.reshape(v.shape[:-1] + (-1, 32))
    amax = np.abs(blocks).max(-1, keepdims=True)
    byte = np.maximum(np.where(amax > 0, np.frexp(amax)[1] - 1 + 127, 0) - down, 1)
    scale = np.exp2(byte - 127.0)
    codes = (blocks / scale).astype(np.float32).astype(dtype).astype(np.float64)
    return np.moveaxis((codes * scale).reshape(v.shape), -1, axis)


WIDE = False


def mx_kscale(k):
    if not WIDE:
        return np.ones(k)
    levels = np.array([10, -10, 5, -5, 0])
    if k % 512:
        return np.exp2(np.random.permutation(np.resize(levels, k // 32))).repeat(32)
    a = np.empty((k // 512, 16))
    for p in range(k // 512):
        a[p, :8] = np.random.permutation(np.resize(levels, 8))
        for g in range(8):
            far = levels[np.abs(levels - a[p, g]) >= 10]
            a[p, g + 8] = far[np.random.randint(len(far))]
    return np.exp2(a.ravel()).repeat(32)


def f64(x):
    return np.asarray(x).astype(np.float64)


def striped(idx):
    return np.tile(idx.reshape(-1, 16).T, (8, 1)).astype(np.uint16)


def unstriped(offs):
    return offs[:16].T.reshape(-1).astype(np.int64)


def striped8(idx):
    return np.concatenate([x.reshape(-1, 16).T for x in idx]).astype(np.uint16)


def runs(offs, k):
    lists = np.stack([offs[16 * r : 16 * r + 16].T.reshape(-1) for r in range(8)]).astype(np.int64)
    return lists[np.arange(k) % 512 // 64]


def pack_weight(w):
    k, n = w.shape
    w = f64(np.asarray(w, np.float32).astype(ml_dtypes.bfloat16)).reshape(k // 32, 32, n)
    amax = np.abs(w).max(1)
    byte = np.clip(np.where(amax > 0, np.frexp(amax)[1] - 1 + 127 - 7, 1), 1, 254)
    scaled = (w * np.exp2(127.0 - byte)[:, None, :]).reshape(k, n).astype(np.float32)
    words = np.ascontiguousarray(scaled.reshape(k // 512, 128, 4, n).transpose(0, 1, 3, 2)).astype(ml_dtypes.float8_e4m3fn).view(np.uint8)
    return words, np.ascontiguousarray(byte.astype(np.uint8).reshape(k // 512, 16, n))


def unpack_weight(words, scales):
    g, p, n, _ = words.shape
    vals = np.ascontiguousarray(words).view(ml_dtypes.float8_e4m3fn).astype(np.float64) * np.repeat(np.exp2(scales.astype(np.float64) - 127.0), 8, axis=1)[..., None]
    return vals.transpose(0, 1, 3, 2).reshape(g * 512, n)


K, T, S, N, H, C = 512, 2048, 512, 512, 512, 512


def setup_inputs():
    n = np.random.standard_normal
    s = mx_kscale(K)[:, None]
    u = mx_kscale(S)
    packed_xT = pack_weight(n((K, T)) * s)
    return {
        "x_words": packed_xT[0],
        "x_scales": packed_xT[1],
        "w1": (n((K, H)) / np.sqrt(K) / s).astype(np.float32),
        "w2": (n((K, H)) / np.sqrt(K) / s).astype(np.float32),
        "gn": (np.random.uniform(0.5, 1.5, (H, 1)) * u[:, None]).astype(np.float32),
        "w3": (n((H, N)) / np.sqrt(H) / u[:, None]).astype(np.float32),
        "gs": (np.random.uniform(0.5, 1.5, (K, 1)) / s).astype(np.float32),
        "offs": striped(np.random.permutation(T)[:S]),
        "two": striped(np.random.permutation(T)[:S]),
        "n1": striped8(np.stack([np.random.permutation(S) for _ in range(8)])),
        "n2": striped8(np.stack([np.random.permutation(S) for _ in range(8)])),
        "n3": striped8(np.stack([np.random.permutation(S) for _ in range(8)])),
        "cand": striped(np.random.permutation(T)[:C]),
        "n4": striped8(np.stack([np.random.permutation(S) for _ in range(8)])),
        "n5": striped8(np.stack([np.random.permutation(S) for _ in range(8)])),
        "n6": striped8(np.stack([np.random.permutation(S) for _ in range(8)])),
    }


def reference(x_words, x_scales, w1, w2, gn, w3, gs, offs, two, n1, n2, n3, cand, n4, n5, n6):
    x_cand = unpack_weight(x_words, x_scales)[:, unstriped(cand)]
    x_two = unpack_weight(x_words, x_scales)[:, unstriped(two)]
    d = mxq(f64(w2), 0, "e4m3").T @ x_two
    z2 = f64(gs) * (d / (np.abs(d[np.arange(H)[:, None], runs(n3, H)]) + 0.5))
    b = 0.0625 * ((x_cand.T @ mxq(z2, 0, "e4m3")))
    xq = unpack_weight(x_words, x_scales)[:, unstriped(offs)]
    y = mxq(f64(w1), 0, "e4m3").T @ xq
    z = f64(gn) * ((np.tanh(y[np.arange(H)[:, None], runs(n1, H)] - y)) * (y[np.arange(H)[:, None], runs(n2, H)]))
    a = mxq(f64(w3), 0, "e4m3").T @ mxq(z, 0, "e4m3")
    return b * (a[np.arange(N)[:, None], runs(n4, N)] - a) + 0.5 * ((b[np.arange(C)[:, None], runs(n6, C)]) * (a[np.arange(N)[:, None], runs(n5, N)] - a))

@@ -1,0 +1,243 @@
+from contextlib import ExitStack
+
+import concourse.mybir as mybir
+
+F32 = mybir.dt.float32
+BF16 = mybir.dt.bfloat16
+I32 = mybir.dt.int32
+U32 = mybir.dt.uint32
+U16 = mybir.dt.uint16
+U8 = mybir.dt.uint8
+FP8X4 = mybir.dt.float8_e4m3fn_x4
+ACT = mybir.ActivationFunctionType
+ALU = mybir.AluOpType
+
+P = 128
+PACK = 4
+T = 2048
+S = 512
+HALF = 256
+U4 = ("V", "V", "V", "V")
+U5 = ("S", "S", "S", "S")
+B6 = ("S", "S", "S", "S")
+FLOPS = 4 * 2 * 512 * 512 * 512
+
+
+def tile_picked_tfcdflowbfdifnorm_none_p_kernel(
+    tc, x_words, x_scales, w1, w2, gn, w3, gs, offs, two, n1, n2, n3, cand, n4, n5, n6, out
+):
+    nc = tc.nc
+    with ExitStack() as ctx:
+        pool = ctx.enter_context(tc.tile_pool(name="held", bufs=1))
+        psum = ctx.enter_context(tc.psum_pool(name="psum", bufs=1))
+
+        def load_list(name, src):
+            lst = pool.tile([P, S // 16], U16, name=name)
+            nc.sync.dma_start(lst[:], src)
+            return lst
+
+        def load_weight(name, w):
+            halves = []
+            for h in range(2):
+                raw = pool.tile([P, PACK, HALF], F32, name=f"{name}_raw{h}")
+                nc.sync.dma_start(raw[:], w.rearrange("(p j) c -> p j c", j=PACK)[:, :, h * HALF : (h + 1) * HALF])
+                halves.append(raw)
+            return halves
+
+        def load_column(name, v):
+            col = pool.tile([P, PACK], F32, name=name)
+            nc.sync.dma_start(col[:], v.rearrange("(p t) o -> p (t o)", t=PACK))
+            return col
+
+        def planes(name):
+            return [pool.tile([P, S], F32, name=f"{name}{t}") for t in range(PACK)]
+
+        def cols(h):
+            return slice(h * HALF, (h + 1) * HALF)
+
+        def look(window, lst, h):
+            return window[:].indirect(lst[:, h * HALF // 16 : (h + 1) * HALF // 16])
+
+        table_scales = pool.tile([P, T], U8, name="table_scales")
+        nc.gpsimd.memset(table_scales[:].bitcast(I32), 0)
+        half_col = pool.tile([P, 1], F32, name="half_col")
+        nc.gpsimd.memset(half_col[:], 0.5)
+
+        offs_l = load_list("offs_l", offs)
+        table_words = pool.tile([P, T], U32, name="table_words")
+        nc.sync.dma_start(table_words[:].bitcast(I32), x_words[0].rearrange("p n r -> p (n r)").bitcast(I32))
+        for q in range(4):
+            nc.sync.dma_start(
+                table_scales[32 * q : 32 * q + 4, :].bitcast(I32), x_scales[0, 4 * q : 4 * q + 4, :].bitcast(I32)
+            )
+        w1_raw = load_weight("w1", w1)
+        two_l = load_list("two_l", two)
+        w2_raw = load_weight("w2", w2)
+        n1_l = load_list("n1_l", n1)
+        w3_raw = load_weight("w3", w3)
+        cand_l = load_list("cand_l", cand)
+        gn_c = load_column("gn_c", gn)
+        n2_l = load_list("n2_l", n2)
+        n3_l = load_list("n3_l", n3)
+        gs_c = load_column("gs_c", gs)
+        n4_l = load_list("n4_l", n4)
+        n5_l = load_list("n5_l", n5)
+        n6_l = load_list("n6_l", n6)
+
+        def gpsimd_round(out, in_):
+            nc.gpsimd.tensor_scalar(out, in_, 1.0, 0.0, ALU.mult, ALU.add)
+
+        def round_weight(name, halves, copies):
+            grouped = pool.tile([P, PACK, P, PACK], BF16, name=f"{name}_grouped", align_bytes=64)
+            for h in range(2):
+                copies[h](
+                    out=grouped[:, :, h * 64 : (h + 1) * 64, :].rearrange("p t m j -> p m t j"),
+                    in_=halves[h][:].rearrange("p j (m t) -> p m t j", t=PACK),
+                )
+            return grouped
+
+        def mx_tiles(name):
+            codes = pool.tile([P, S], U32, name=f"{name}_codes", align_bytes=64)
+            scales = pool.tile([P, S], U8, name=f"{name}_scales", align_bytes=64)
+            return codes, scales
+
+        def quantize_weight(name, grouped):
+            codes, scales = mx_tiles(name)
+            nc.vector.quantize_mx(
+                out=codes[:].bitcast(FP8X4), scales=scales[:], in_=grouped[:].rearrange("p t m j -> p (t m j)")
+            )
+            return codes, scales
+
+        def gather_tokens(name, lst, view):
+            codes, scales = mx_tiles(name)
+            nc.vector.tensor_copy(view(codes[:]), table_words[:].indirect(lst[:]))
+            nc.vector.tensor_copy(view(scales[:]), table_scales[:].indirect(lst[:]))
+            return codes, scales
+
+        def product(banks, stationary, moving, n_cols):
+            for t in range(PACK):
+                m_cols = slice(t * P, (t + 1) * P)
+                nc.tensor.matmul_mx(
+                    out=banks[t][:, n_cols],
+                    lhsT=stationary[0][:, m_cols].bitcast(FP8X4),
+                    lhsT_scale=stationary[1][:, m_cols],
+                    rhs=moving[0][:, n_cols].bitcast(FP8X4),
+                    rhs_scale=moving[1][:, n_cols],
+                    start=True,
+                    stop=True,
+                )
+
+        def quantize_half(rows, grouped, mx, h):
+            nc.vector.tensor_copy(
+                out=grouped[:, cols(h), :].rearrange("p (c i) t -> p c t i", i=4),
+                in_=rows[:, :, cols(h)].rearrange("p t (c i) -> p c t i", i=4),
+            )
+            nc.vector.quantize_mx(
+                out=mx[0][:, cols(h)].bitcast(FP8X4),
+                scales=mx[1][:, cols(h)],
+                in_=grouped[:, cols(h), :].rearrange("p s t -> p (s t)"),
+            )
+
+        ya_banks = [psum.tile([P, S], F32, name=f"ya_bank{t}") for t in range(PACK)]
+        db_banks = [psum.tile([P, S], F32, name=f"db_bank{t}") for t in range(PACK)]
+        whole = slice(0, S)
+
+        xq = gather_tokens("xq", offs_l, lambda ap: ap)
+        w1_grouped = round_weight("w1", w1_raw, (nc.scalar.copy, nc.scalar.copy))
+        w1_mx = quantize_weight("w1", w1_grouped)
+        product(ya_banks, w1_mx, xq, whole)
+
+        y_win = planes("y_win")
+        y_own = planes("y_own")
+        for t in range(PACK):
+            nc.scalar.copy(out=y_win[t][:], in_=ya_banks[t][:])
+            if t < 0:
+                nc.vector.tensor_copy(y_own[t][:], y_win[t][:])
+            else:
+                nc.sync.dma_start(y_own[t][:], y_win[t][:])
+
+        x_two = gather_tokens("x_two", two_l, lambda ap: ap)
+        w2_grouped = round_weight("w2", w2_raw, (nc.scalar.copy, nc.vector.tensor_copy))
+        w2_mx = quantize_weight("w2", w2_grouped)
+        product(db_banks, w2_mx, x_two, whole)
+
+        x_cand = gather_tokens("x_cand", cand_l, lambda ap: ap.rearrange("p (t m) -> p m t", t=PACK))
+
+        log_den = planes("log_den")
+        for t in range(PACK):
+            nc.scalar.activation(out=log_den[t][:], in_=db_banks[t][:], func=ACT.Abs)
+        for t in range(PACK):
+            nc.scalar.activation(out=log_den[t][:], in_=log_den[t][:], func=ACT.Ln, bias=half_col[:])
+
+        w3_grouped = round_weight("w3", w3_raw, (nc.vector.tensor_copy, nc.vector.tensor_copy))
+        w3_mx = quantize_weight("w3", w3_grouped)
+
+        y_diff = planes("y_diff")
+        for t in range(PACK):
+            for h in range(2):
+                nc.vector.tensor_tensor(y_diff[t][:, cols(h)], look(y_win[t], n1_l, h), y_own[t][:, cols(h)], ALU.subtract)
+
+        y_gain = planes("y_gain")
+        z_rows = pool.tile([P, PACK, S], F32, name="z_rows")
+        for t in range(PACK):
+            nc.scalar.activation(out=y_gain[t][:], in_=ya_banks[t][:], func=ACT.Copy, scale=gn_c[:, t : t + 1])
+            nc.scalar.activation(out=y_diff[t][:], in_=y_diff[t][:], func=ACT.Tanh)
+            for h in range(2):
+                nc.vector.tensor_tensor(z_rows[:, t, cols(h)], look(y_gain[t], n2_l, h), y_diff[t][:, cols(h)], ALU.mult)
+
+        z_grouped = pool.tile([P, S, PACK], BF16, name="z_grouped", align_bytes=64)
+        z_mx = mx_tiles("z")
+        for h in range(2):
+            quantize_half(z_rows, z_grouped, z_mx, h)
+            product(ya_banks, w3_mx, z_mx, cols(h))
+
+        inv_den = planes("inv_den")
+        z2_rows = pool.tile([P, PACK, S], F32, name="z2_rows")
+        for t in range(PACK):
+            for h in range(2):
+                nc.scalar.activation(out=inv_den[t][:, cols(h)], in_=look(log_den[t], n3_l, h), func=ACT.Exp, scale=-1.0)
+            nc.vector.scalar_tensor_tensor(
+                z2_rows[:, t, :], db_banks[t][:], gs_c[:, t : t + 1], inv_den[t][:], ALU.mult, ALU.mult
+            )
+
+        a_win = planes("a_win")
+        a_own = planes("a_own")
+        for t in range(PACK):
+            nc.scalar.copy(out=a_win[t][:], in_=ya_banks[t][:])
+            if "V" in (U4[t], U5[t]):
+                nc.sync.dma_start(a_own[t][:], a_win[t][:])
+
+        z2_grouped = pool.tile([P, S, PACK], BF16, name="z2_grouped", align_bytes=64)
+        z2_mx = mx_tiles("z2")
+        for h in range(2):
+            quantize_half(z2_rows, z2_grouped, z2_mx, h)
+            product(db_banks, x_cand, z2_mx, cols(h))
+
+        first = planes("first")
+        second = planes("second")
+        b_win = planes("b_win")
+        b_far = planes("b_far")
+        out_rows = out.rearrange("(p t) s -> p t s", t=PACK)
+        def diff(dst, lst, who, t):
+            for h in range(2):
+                if who == "S":
+                    nc.scalar.activation(out=dst[:, cols(h)], in_=look(a_win[t], lst, h), func=ACT.Copy)
+                else:
+                    nc.vector.tensor_tensor(dst[:, cols(h)], look(a_win[t], lst, h), a_own[t][:, cols(h)], ALU.subtract)
+            if who == "S":
+                nc.vector.tensor_tensor(dst[:], dst[:], ya_banks[t][:], ALU.subtract)
+
+        for t in range(PACK):
+            diff(second[t], n5_l, U5[t], t)
+            diff(first[t], n4_l, U4[t], t)
+            nc.scalar.activation(out=b_win[t][:], in_=db_banks[t][:], func=ACT.Copy, scale=0.03125)
+            for h in range(2):
+                if B6[t] == "S":
+                    nc.scalar.activation(out=b_far[t][:, cols(h)], in_=look(b_win[t], n6_l, h), func=ACT.Copy)
+                else:
+                    nc.vector.tensor_tensor(b_far[t][:, cols(h)], look(b_win[t], n6_l, h), second[t][:, cols(h)], ALU.mult)
+            nc.vector.scalar_tensor_tensor(first[t][:], db_banks[t][:], 0.0625, first[t][:], ALU.mult, ALU.mult)
+            if B6[t] == "S":
+                nc.vector.tensor_tensor(b_far[t][:], second[t][:], b_far[t][:], ALU.mult)
+            nc.vector.tensor_tensor(first[t][:], first[t][:], b_far[t][:], ALU.add)
+            nc.sync.dma_start(out_rows[:, t, :], first[t][:])

@@ -17,8 +17,8 @@ PACK = 4
 T = 2048
 S = 512
 HALF = 256
-U4 = ("V", "V", "V", "V")
-U5 = ("S", "S", "S", "S")
+U4 = ("V", "V", "S", "S")
+U5 = ("V", "S", "S", "S")
 B6 = ("S", "S", "S", "S")
 FLOPS = 4 * 2 * 512 * 512 * 512
 
@@ -29,6 +29,7 @@ def tile_picked_tfcdflowbfdifnorm_none_p_kernel(
     nc = tc.nc
     with ExitStack() as ctx:
         pool = ctx.enter_context(tc.tile_pool(name="held", bufs=1))
+        reuse = ctx.enter_context(tc.tile_pool(name="reuse", bufs=1))
         psum = ctx.enter_context(tc.psum_pool(name="psum", bufs=1))
 
         def load_list(name, src):
@@ -55,28 +56,27 @@ def tile_picked_tfcdflowbfdifnorm_none_p_kernel(
         def cols(h):
             return slice(h * HALF, (h + 1) * HALF)
 
-        def look(window, lst, h):
-            return window[:].indirect(lst[:, h * HALF // 16 : (h + 1) * HALF // 16])
-
         table_scales = pool.tile([P, T], U8, name="table_scales")
         nc.gpsimd.memset(table_scales[:].bitcast(I32), 0)
         half_col = pool.tile([P, 1], F32, name="half_col")
         nc.gpsimd.memset(half_col[:], 0.5)
 
+        warm = pool.tile([P, 1], F32, name="warm")
+        nc.scalar.activation(out=warm[:], in_=half_col[:], func=ACT.Ln)
         offs_l = load_list("offs_l", offs)
-        table_words = pool.tile([P, T], U32, name="table_words")
-        nc.sync.dma_start(table_words[:].bitcast(I32), x_words[0].rearrange("p n r -> p (n r)").bitcast(I32))
         for q in range(4):
             nc.sync.dma_start(
                 table_scales[32 * q : 32 * q + 4, :].bitcast(I32), x_scales[0, 4 * q : 4 * q + 4, :].bitcast(I32)
             )
-        w1_raw = load_weight("w1", w1)
         two_l = load_list("two_l", two)
+        cand_l = load_list("cand_l", cand)
+        table_words = pool.tile([P, T], U32, name="table_words")
+        nc.sync.dma_start(table_words[:].bitcast(I32), x_words[0].rearrange("p n r -> p (n r)").bitcast(I32))
+        w1_raw = load_weight("w1", w1)
+        gn_c = load_column("gn_c", gn)
         w2_raw = load_weight("w2", w2)
         n1_l = load_list("n1_l", n1)
         w3_raw = load_weight("w3", w3)
-        cand_l = load_list("cand_l", cand)
-        gn_c = load_column("gn_c", gn)
         n2_l = load_list("n2_l", n2)
         n3_l = load_list("n3_l", n3)
         gs_c = load_column("gs_c", gs)
@@ -88,7 +88,12 @@ def tile_picked_tfcdflowbfdifnorm_none_p_kernel(
             nc.gpsimd.tensor_scalar(out, in_, 1.0, 0.0, ALU.mult, ALU.add)
 
         def round_weight(name, halves, copies):
-            grouped = pool.tile([P, PACK, P, PACK], BF16, name=f"{name}_grouped", align_bytes=64)
+            if name == "w2":
+                grouped = reuse.tile([P, PACK, P, PACK], BF16, name=f"{name}_grouped", offset=0, align_bytes=64)
+            elif name == "w3":
+                grouped = reuse.tile([P, PACK, P, PACK], BF16, name=f"{name}_grouped", offset=2560, align_bytes=64)
+            else:
+                grouped = pool.tile([P, PACK, P, PACK], BF16, name=f"{name}_grouped", tag=f"{name}_grouped", align_bytes=64)
             for h in range(2):
                 copies[h](
                     out=grouped[:, :, h * 64 : (h + 1) * 64, :].rearrange("p t m j -> p m t j"),
@@ -96,9 +101,9 @@ def tile_picked_tfcdflowbfdifnorm_none_p_kernel(
                 )
             return grouped
 
-        def mx_tiles(name):
+        def mx_tiles(name, over=None):
             codes = pool.tile([P, S], U32, name=f"{name}_codes", align_bytes=64)
-            scales = pool.tile([P, S], U8, name=f"{name}_scales", align_bytes=64)
+            scales = pool.tile([P, S], U8, name=f"{name}_scales", tag=over or f"{name}_scales", align_bytes=64)
             return codes, scales
 
         def quantize_weight(name, grouped):
@@ -108,11 +113,11 @@ def tile_picked_tfcdflowbfdifnorm_none_p_kernel(
             )
             return codes, scales
 
-        def gather_tokens(name, lst, view):
-            codes, scales = mx_tiles(name)
-            nc.vector.tensor_copy(view(codes[:]), table_words[:].indirect(lst[:]))
-            nc.vector.tensor_copy(view(scales[:]), table_scales[:].indirect(lst[:]))
-            return codes, scales
+        def deal(dst, src, run):
+            nc.vector.tensor_copy(
+                dst[:].rearrange("p (t g r) -> p g t r", t=PACK, r=run),
+                src[:].rearrange("p (g r t) -> p g t r", t=PACK, r=run),
+            )
 
         def product(banks, stationary, moving, n_cols):
             for t in range(PACK):
@@ -127,8 +132,8 @@ def tile_picked_tfcdflowbfdifnorm_none_p_kernel(
                     stop=True,
                 )
 
-        def quantize_half(rows, grouped, mx, h):
-            nc.vector.tensor_copy(
+        def quantize_half(rows, grouped, mx, h, copy):
+            copy(
                 out=grouped[:, cols(h), :].rearrange("p (c i) t -> p c t i", i=4),
                 in_=rows[:, :, cols(h)].rearrange("p t (c i) -> p c t i", i=4),
             )
@@ -142,102 +147,112 @@ def tile_picked_tfcdflowbfdifnorm_none_p_kernel(
         db_banks = [psum.tile([P, S], F32, name=f"db_bank{t}") for t in range(PACK)]
         whole = slice(0, S)
 
-        xq = gather_tokens("xq", offs_l, lambda ap: ap)
+        xq = mx_tiles("xq")
+        x_two = mx_tiles("x_two")
+        nc.vector.tensor_copy(xq[1][:], table_scales[:].indirect(offs_l[:]))
+        nc.vector.tensor_copy(x_two[1][:], table_scales[:].indirect(two_l[:]))
+        listed_scales = pool.tile([P, S], U8, name="listed_scales", align_bytes=64)
+        nc.vector.tensor_copy(listed_scales[:], table_scales[:].indirect(cand_l[:]))
         w1_grouped = round_weight("w1", w1_raw, (nc.scalar.copy, nc.scalar.copy))
         w1_mx = quantize_weight("w1", w1_grouped)
+        nc.vector.tensor_copy(xq[0][:], table_words[:].indirect(offs_l[:]))
         product(ya_banks, w1_mx, xq, whole)
+        nc.vector.tensor_copy(x_two[0][:], table_words[:].indirect(two_l[:]))
 
-        y_win = planes("y_win")
-        y_own = planes("y_own")
-        for t in range(PACK):
-            nc.scalar.copy(out=y_win[t][:], in_=ya_banks[t][:])
-            if t < 0:
-                nc.vector.tensor_copy(y_own[t][:], y_win[t][:])
-            else:
-                nc.sync.dma_start(y_own[t][:], y_win[t][:])
-
-        x_two = gather_tokens("x_two", two_l, lambda ap: ap)
         w2_grouped = round_weight("w2", w2_raw, (nc.scalar.copy, nc.vector.tensor_copy))
+        ya_win = [pool.tile([P, 2 * S], F32, name=f"ya_win{t}") for t in range(PACK)]
+        db_win = [pool.tile([P, 2 * S], F32, name=f"db_win{t}") for t in range(PACK)]
+        own = [db_win[t][:, S:] for t in range(PACK)]
+        gn_inv = pool.tile([P, PACK], F32, name="gn_inv", tag="after_tanh")
+        nc.vector.scalar_tensor_tensor(gn_inv[:], gn_c[:], -1.0, gn_c[:], ALU.mult, ALU.max)
+        nc.vector.scalar_tensor_tensor(gn_inv[:], gn_inv[:], 2.0**-120, gn_c[:], ALU.is_lt, ALU.add)
+        nc.vector.reciprocal(gn_inv[:], gn_inv[:])
+        for t in range(PACK):
+            nc.scalar.activation(out=ya_win[t][:, :S], in_=ya_banks[t][:], func=ACT.Copy, scale=gn_c[:, t : t + 1])
+            nc.sync.dma_start(own[t], ya_win[t][:, :S])
+
         w2_mx = quantize_weight("w2", w2_grouped)
         product(db_banks, w2_mx, x_two, whole)
 
-        x_cand = gather_tokens("x_cand", cand_l, lambda ap: ap.rearrange("p (t m) -> p m t", t=PACK))
+        listed_codes = reuse.tile([P, S], U32, name="listed_codes", offset=0, align_bytes=64)
+        nc.vector.tensor_copy(listed_codes[:], table_words[:].indirect(cand_l[:]))
+        cand_codes = pool.tile([P, S], U32, name="cand_codes", align_bytes=64)
+        cand_scales = reuse.tile([P, S], U8, name="cand_scales", offset=2048, align_bytes=64)
+        deal(cand_scales, listed_scales, 16)
+        deal(cand_codes, listed_codes, 4)
+        x_cand = (cand_codes, cand_scales)
 
-        log_den = planes("log_den")
         for t in range(PACK):
-            nc.scalar.activation(out=log_den[t][:], in_=db_banks[t][:], func=ACT.Abs)
+            nc.scalar.activation(out=ya_win[t][:, S:], in_=db_banks[t][:], func=ACT.Abs)
         for t in range(PACK):
-            nc.scalar.activation(out=log_den[t][:], in_=log_den[t][:], func=ACT.Ln, bias=half_col[:])
+            nc.scalar.activation(out=db_win[t][:, :S], in_=ya_win[t][:, S:], func=ACT.Ln, bias=half_col[:])
+
+        y_diff = planes("y_diff")
+        for t in range(PACK):
+            nc.vector.tensor_tensor(y_diff[t][:], ya_win[t][:].indirect(n1_l[:]), own[t], ALU.subtract)
 
         w3_grouped = round_weight("w3", w3_raw, (nc.vector.tensor_copy, nc.vector.tensor_copy))
         w3_mx = quantize_weight("w3", w3_grouped)
 
-        y_diff = planes("y_diff")
-        for t in range(PACK):
-            for h in range(2):
-                nc.vector.tensor_tensor(y_diff[t][:, cols(h)], look(y_win[t], n1_l, h), y_own[t][:, cols(h)], ALU.subtract)
-
-        y_gain = planes("y_gain")
         z_rows = pool.tile([P, PACK, S], F32, name="z_rows")
         for t in range(PACK):
-            nc.scalar.activation(out=y_gain[t][:], in_=ya_banks[t][:], func=ACT.Copy, scale=gn_c[:, t : t + 1])
-            nc.scalar.activation(out=y_diff[t][:], in_=y_diff[t][:], func=ACT.Tanh)
-            for h in range(2):
-                nc.vector.tensor_tensor(z_rows[:, t, cols(h)], look(y_gain[t], n2_l, h), y_diff[t][:, cols(h)], ALU.mult)
+            nc.scalar.activation(out=y_diff[t][:], in_=y_diff[t][:], func=ACT.Tanh, scale=gn_inv[:, t : t + 1])
+            if t < 4:
+                nc.vector.tensor_tensor(z_rows[:, t, :], ya_win[t][:].indirect(n2_l[:]), y_diff[t][:], ALU.mult)
+        for t in range(4, PACK):
+            y_far = pool.tile([P, S], F32, name="y_far", tag="after_tanh")
+            nc.scalar.activation(out=y_far[:], in_=ya_win[t][:].indirect(n2_l[:]), func=ACT.Copy)
+            nc.vector.tensor_tensor(z_rows[:, t, :], y_far[:], y_diff[t][:], ALU.mult)
 
         z_grouped = pool.tile([P, S, PACK], BF16, name="z_grouped", align_bytes=64)
         z_mx = mx_tiles("z")
         for h in range(2):
-            quantize_half(z_rows, z_grouped, z_mx, h)
+            quantize_half(z_rows, z_grouped, z_mx, h, (nc.vector.tensor_copy, nc.vector.tensor_copy)[h])
             product(ya_banks, w3_mx, z_mx, cols(h))
 
-        inv_den = planes("inv_den")
+        inv_den = y_diff
         z2_rows = pool.tile([P, PACK, S], F32, name="z2_rows")
         for t in range(PACK):
-            for h in range(2):
-                nc.scalar.activation(out=inv_den[t][:, cols(h)], in_=look(log_den[t], n3_l, h), func=ACT.Exp, scale=-1.0)
+            nc.scalar.activation(out=inv_den[t][:], in_=db_win[t][:].indirect(n3_l[:]), func=ACT.Exp, scale=-1.0)
             nc.vector.scalar_tensor_tensor(
                 z2_rows[:, t, :], db_banks[t][:], gs_c[:, t : t + 1], inv_den[t][:], ALU.mult, ALU.mult
             )
 
-        a_win = planes("a_win")
-        a_own = planes("a_own")
         for t in range(PACK):
-            nc.scalar.copy(out=a_win[t][:], in_=ya_banks[t][:])
+            nc.scalar.copy(out=ya_win[t][:, :S], in_=ya_banks[t][:])
             if "V" in (U4[t], U5[t]):
-                nc.sync.dma_start(a_own[t][:], a_win[t][:])
+                nc.sync.dma_start(own[t], ya_win[t][:, :S])
 
         z2_grouped = pool.tile([P, S, PACK], BF16, name="z2_grouped", align_bytes=64)
         z2_mx = mx_tiles("z2")
         for h in range(2):
-            quantize_half(z2_rows, z2_grouped, z2_mx, h)
+            quantize_half(z2_rows, z2_grouped, z2_mx, h, (nc.vector.tensor_copy, nc.vector.tensor_copy)[h])
             product(db_banks, x_cand, z2_mx, cols(h))
 
         first = planes("first")
         second = planes("second")
-        b_win = planes("b_win")
         b_far = planes("b_far")
         out_rows = out.rearrange("(p t) s -> p t s", t=PACK)
+
         def diff(dst, lst, who, t):
-            for h in range(2):
-                if who == "S":
-                    nc.scalar.activation(out=dst[:, cols(h)], in_=look(a_win[t], lst, h), func=ACT.Copy)
-                else:
-                    nc.vector.tensor_tensor(dst[:, cols(h)], look(a_win[t], lst, h), a_own[t][:, cols(h)], ALU.subtract)
             if who == "S":
+                nc.scalar.activation(out=dst[:], in_=ya_win[t][:].indirect(lst[:]), func=ACT.Copy)
                 nc.vector.tensor_tensor(dst[:], dst[:], ya_banks[t][:], ALU.subtract)
+            else:
+                nc.vector.tensor_tensor(dst[:], ya_win[t][:].indirect(lst[:]), own[t], ALU.subtract)
 
         for t in range(PACK):
-            diff(second[t], n5_l, U5[t], t)
             diff(first[t], n4_l, U4[t], t)
-            nc.scalar.activation(out=b_win[t][:], in_=db_banks[t][:], func=ACT.Copy, scale=0.03125)
-            for h in range(2):
-                if B6[t] == "S":
-                    nc.scalar.activation(out=b_far[t][:, cols(h)], in_=look(b_win[t], n6_l, h), func=ACT.Copy)
-                else:
-                    nc.vector.tensor_tensor(b_far[t][:, cols(h)], look(b_win[t], n6_l, h), second[t][:, cols(h)], ALU.mult)
+            diff(second[t], n5_l, U5[t], t)
+            nc.scalar.activation(out=db_win[t][:, :S], in_=db_banks[t][:], func=ACT.Copy, scale=0.03125)
             nc.vector.scalar_tensor_tensor(first[t][:], db_banks[t][:], 0.0625, first[t][:], ALU.mult, ALU.mult)
             if B6[t] == "S":
-                nc.vector.tensor_tensor(b_far[t][:], second[t][:], b_far[t][:], ALU.mult)
-            nc.vector.tensor_tensor(first[t][:], first[t][:], b_far[t][:], ALU.add)
-            nc.sync.dma_start(out_rows[:, t, :], first[t][:])
+                nc.scalar.activation(out=b_far[t][:], in_=db_win[t][:].indirect(n6_l[:]), func=ACT.Copy)
+            else:
+                nc.vector.tensor_tensor(b_far[t][:], db_win[t][:].indirect(n6_l[:]), second[t][:], ALU.mult)
+            for part in (cols(0), cols(1)) if t == PACK - 1 else (whole,):
+                if B6[t] == "S":
+                    nc.vector.tensor_tensor(b_far[t][:, part], second[t][:, part], b_far[t][:, part], ALU.mult)
+            for part in (cols(0), cols(1)) if t == PACK - 1 else (whole,):
+                nc.vector.tensor_tensor(first[t][:, part], first[t][:, part], b_far[t][:, part], ALU.add)
+                nc.sync.dma_start(out_rows[:, t, part], first[t][:, part])

@@ -16,11 +16,13 @@ P = 128
 PACK = 4
 T = 2048
 S = 512
-HALF = 256
-U4 = ("V", "V", "S", "S")
-U5 = ("V", "S", "S", "S")
-B6 = ("S", "S", "S", "S")
-FLOPS = 4 * 2 * 512 * 512 * 512
+HALF = S // 2
+PER_COLUMN = 16
+LINE = 16
+TINY_GAIN = 2.0**-120
+N4_TILES_ON_VECTOR = 2
+N5_TILES_ON_VECTOR = 1
+FLOPS = 4 * 2 * S * S * S
 
 
 def tile_picked_tfcdflowbfdifnorm_none_p_kernel(
@@ -32,79 +34,42 @@ def tile_picked_tfcdflowbfdifnorm_none_p_kernel(
         reuse = ctx.enter_context(tc.tile_pool(name="reuse", bufs=1))
         psum = ctx.enter_context(tc.psum_pool(name="psum", bufs=1))
 
+        halves = (slice(0, HALF), slice(HALF, S))
+        whole = slice(0, S)
+
         def load_list(name, src):
-            lst = pool.tile([P, S // 16], U16, name=name)
+            lst = pool.tile([P, S // PER_COLUMN], U16, name=name)
             nc.sync.dma_start(lst[:], src)
             return lst
 
         def load_weight(name, w):
-            halves = []
-            for h in range(2):
+            raws = []
+            for h, part in enumerate(halves):
                 raw = pool.tile([P, PACK, HALF], F32, name=f"{name}_raw{h}")
-                nc.sync.dma_start(raw[:], w.rearrange("(p j) c -> p j c", j=PACK)[:, :, h * HALF : (h + 1) * HALF])
-                halves.append(raw)
-            return halves
+                nc.sync.dma_start(raw[:], w.rearrange("(p j) c -> p j c", j=PACK)[:, :, part])
+                raws.append(raw)
+            return raws
 
-        def load_column(name, v):
+        def load_gain(name, gain):
             col = pool.tile([P, PACK], F32, name=name)
-            nc.sync.dma_start(col[:], v.rearrange("(p t) o -> p (t o)", t=PACK))
+            nc.sync.dma_start(col[:], gain.rearrange("(p t) o -> p (t o)", t=PACK))
             return col
 
-        def planes(name):
-            return [pool.tile([P, S], F32, name=f"{name}{t}") for t in range(PACK)]
+        def row_tiles(name, width):
+            return [pool.tile([P, width], F32, name=f"{name}{t}") for t in range(PACK)]
 
-        def cols(h):
-            return slice(h * HALF, (h + 1) * HALF)
+        def mx_tiles(name):
+            codes = pool.tile([P, S], U32, name=f"{name}_codes", align_bytes=64)
+            scales = pool.tile([P, S], U8, name=f"{name}_scales", align_bytes=64)
+            return codes, scales
 
-        table_scales = pool.tile([P, T], U8, name="table_scales")
-        nc.gpsimd.memset(table_scales[:].bitcast(I32), 0)
-        half_col = pool.tile([P, 1], F32, name="half_col")
-        nc.gpsimd.memset(half_col[:], 0.5)
-
-        warm = pool.tile([P, 1], F32, name="warm")
-        nc.scalar.activation(out=warm[:], in_=half_col[:], func=ACT.Ln)
-        offs_l = load_list("offs_l", offs)
-        for q in range(4):
-            nc.sync.dma_start(
-                table_scales[32 * q : 32 * q + 4, :].bitcast(I32), x_scales[0, 4 * q : 4 * q + 4, :].bitcast(I32)
-            )
-        two_l = load_list("two_l", two)
-        cand_l = load_list("cand_l", cand)
-        table_words = pool.tile([P, T], U32, name="table_words")
-        nc.sync.dma_start(table_words[:].bitcast(I32), x_words[0].rearrange("p n r -> p (n r)").bitcast(I32))
-        w1_raw = load_weight("w1", w1)
-        gn_c = load_column("gn_c", gn)
-        w2_raw = load_weight("w2", w2)
-        n1_l = load_list("n1_l", n1)
-        w3_raw = load_weight("w3", w3)
-        n2_l = load_list("n2_l", n2)
-        n3_l = load_list("n3_l", n3)
-        gs_c = load_column("gs_c", gs)
-        n4_l = load_list("n4_l", n4)
-        n5_l = load_list("n5_l", n5)
-        n6_l = load_list("n6_l", n6)
-
-        def gpsimd_round(out, in_):
-            nc.gpsimd.tensor_scalar(out, in_, 1.0, 0.0, ALU.mult, ALU.add)
-
-        def round_weight(name, halves, copies):
-            if name == "w2":
-                grouped = reuse.tile([P, PACK, P, PACK], BF16, name=f"{name}_grouped", offset=0, align_bytes=64)
-            elif name == "w3":
-                grouped = reuse.tile([P, PACK, P, PACK], BF16, name=f"{name}_grouped", offset=2560, align_bytes=64)
-            else:
-                grouped = pool.tile([P, PACK, P, PACK], BF16, name=f"{name}_grouped", tag=f"{name}_grouped", align_bytes=64)
+        def round_weight(grouped, raws, copies):
+            m_half = HALF // PACK
             for h in range(2):
                 copies[h](
-                    out=grouped[:, :, h * 64 : (h + 1) * 64, :].rearrange("p t m j -> p m t j"),
-                    in_=halves[h][:].rearrange("p j (m t) -> p m t j", t=PACK),
+                    out=grouped[:, :, h * m_half : (h + 1) * m_half, :].rearrange("p t m j -> p m t j"),
+                    in_=raws[h][:].rearrange("p j (m t) -> p m t j", t=PACK),
                 )
-            return grouped
-
-        def mx_tiles(name, over=None):
-            codes = pool.tile([P, S], U32, name=f"{name}_codes", align_bytes=64)
-            scales = pool.tile([P, S], U8, name=f"{name}_scales", tag=over or f"{name}_scales", align_bytes=64)
-            return codes, scales
 
         def quantize_weight(name, grouped):
             codes, scales = mx_tiles(name)
@@ -132,40 +97,72 @@ def tile_picked_tfcdflowbfdifnorm_none_p_kernel(
                     stop=True,
                 )
 
-        def quantize_half(rows, grouped, mx, h, copy):
-            copy(
-                out=grouped[:, cols(h), :].rearrange("p (c i) t -> p c t i", i=4),
-                in_=rows[:, :, cols(h)].rearrange("p t (c i) -> p c t i", i=4),
+        def quantize_rows(rows, grouped, mx, part):
+            nc.vector.tensor_copy(
+                out=grouped[:, part, :].rearrange("p (c i) t -> p c t i", i=4),
+                in_=rows[:, :, part].rearrange("p t (c i) -> p c t i", i=4),
             )
             nc.vector.quantize_mx(
-                out=mx[0][:, cols(h)].bitcast(FP8X4),
-                scales=mx[1][:, cols(h)],
-                in_=grouped[:, cols(h), :].rearrange("p s t -> p (s t)"),
+                out=mx[0][:, part].bitcast(FP8X4),
+                scales=mx[1][:, part],
+                in_=grouped[:, part, :].rearrange("p s t -> p (s t)"),
             )
+
+        table_scales = pool.tile([P, T], U8, name="table_scales")
+        nc.gpsimd.memset(table_scales[:].bitcast(I32), 0)
+        half_col = pool.tile([P, 1], F32, name="half_col")
+        nc.gpsimd.memset(half_col[:], 0.5)
+
+        warm = pool.tile([P, 1], F32, name="warm")
+        nc.scalar.activation(out=warm[:], in_=half_col[:], func=ACT.Ln)
+
+        offs_l = load_list("offs_l", offs)
+        for q in range(4):
+            nc.sync.dma_start(
+                table_scales[32 * q : 32 * q + 4, :].bitcast(I32), x_scales[0, 4 * q : 4 * q + 4, :].bitcast(I32)
+            )
+        two_l = load_list("two_l", two)
+        w1_raw = load_weight("w1", w1)
+        cand_l = load_list("cand_l", cand)
+        table_words = pool.tile([P, T], U32, name="table_words")
+        nc.sync.dma_start(table_words[:].bitcast(I32), x_words[0].rearrange("p n r -> p (n r)").bitcast(I32))
+        w2_raw = load_weight("w2", w2)
+        gn_c = load_gain("gn_c", gn)
+        n1_l = load_list("n1_l", n1)
+        w3_raw = load_weight("w3", w3)
+        n2_l = load_list("n2_l", n2)
+        n3_l = load_list("n3_l", n3)
+        gs_c = load_gain("gs_c", gs)
+        n4_l = load_list("n4_l", n4)
+        n5_l = load_list("n5_l", n5)
+        n6_l = load_list("n6_l", n6)
 
         ya_banks = [psum.tile([P, S], F32, name=f"ya_bank{t}") for t in range(PACK)]
         db_banks = [psum.tile([P, S], F32, name=f"db_bank{t}") for t in range(PACK)]
-        whole = slice(0, S)
 
-        xq = mx_tiles("xq")
+        x_offs = mx_tiles("x_offs")
         x_two = mx_tiles("x_two")
-        nc.vector.tensor_copy(xq[1][:], table_scales[:].indirect(offs_l[:]))
+        nc.vector.tensor_copy(x_offs[1][:], table_scales[:].indirect(offs_l[:]))
         nc.vector.tensor_copy(x_two[1][:], table_scales[:].indirect(two_l[:]))
         listed_scales = pool.tile([P, S], U8, name="listed_scales", align_bytes=64)
         nc.vector.tensor_copy(listed_scales[:], table_scales[:].indirect(cand_l[:]))
-        w1_grouped = round_weight("w1", w1_raw, (nc.scalar.copy, nc.scalar.copy))
+        w1_grouped = pool.tile([P, PACK, P, PACK], BF16, name="w1_grouped", align_bytes=64)
+        round_weight(w1_grouped, w1_raw, (nc.scalar.copy, nc.scalar.copy))
         w1_mx = quantize_weight("w1", w1_grouped)
-        nc.vector.tensor_copy(xq[0][:], table_words[:].indirect(offs_l[:]))
-        product(ya_banks, w1_mx, xq, whole)
+        nc.vector.tensor_copy(x_offs[0][:], table_words[:].indirect(offs_l[:]))
+        product(ya_banks, w1_mx, x_offs, whole)
         nc.vector.tensor_copy(x_two[0][:], table_words[:].indirect(two_l[:]))
 
-        w2_grouped = round_weight("w2", w2_raw, (nc.scalar.copy, nc.vector.tensor_copy))
-        ya_win = [pool.tile([P, 2 * S], F32, name=f"ya_win{t}") for t in range(PACK)]
-        db_win = [pool.tile([P, 2 * S], F32, name=f"db_win{t}") for t in range(PACK)]
+        w2_grouped = reuse.tile([P, PACK, P, PACK], BF16, name="w2_grouped", offset=0, align_bytes=64)
+        round_weight(w2_grouped, w2_raw, (nc.scalar.copy, nc.vector.tensor_copy))
+
+        ya_win = row_tiles("ya_win", 2 * S)
+        db_win = row_tiles("db_win", 2 * S)
         own = [db_win[t][:, S:] for t in range(PACK)]
-        gn_inv = pool.tile([P, PACK], F32, name="gn_inv", tag="after_tanh")
+
+        gn_inv = pool.tile([P, PACK], F32, name="gn_inv")
         nc.vector.scalar_tensor_tensor(gn_inv[:], gn_c[:], -1.0, gn_c[:], ALU.mult, ALU.max)
-        nc.vector.scalar_tensor_tensor(gn_inv[:], gn_inv[:], 2.0**-120, gn_c[:], ALU.is_lt, ALU.add)
+        nc.vector.scalar_tensor_tensor(gn_inv[:], gn_inv[:], TINY_GAIN, gn_c[:], ALU.is_lt, ALU.add)
         nc.vector.reciprocal(gn_inv[:], gn_inv[:])
         for t in range(PACK):
             nc.scalar.activation(out=ya_win[t][:, :S], in_=ya_banks[t][:], func=ACT.Copy, scale=gn_c[:, t : t + 1])
@@ -177,82 +174,76 @@ def tile_picked_tfcdflowbfdifnorm_none_p_kernel(
         listed_codes = reuse.tile([P, S], U32, name="listed_codes", offset=0, align_bytes=64)
         nc.vector.tensor_copy(listed_codes[:], table_words[:].indirect(cand_l[:]))
         cand_codes = pool.tile([P, S], U32, name="cand_codes", align_bytes=64)
-        cand_scales = reuse.tile([P, S], U8, name="cand_scales", offset=2048, align_bytes=64)
-        deal(cand_scales, listed_scales, 16)
-        deal(cand_codes, listed_codes, 4)
-        x_cand = (cand_codes, cand_scales)
+        cand_scales = reuse.tile([P, S], U8, name="cand_scales", offset=4 * S, align_bytes=64)
+        deal(cand_scales, listed_scales, LINE)
+        deal(cand_codes, listed_codes, LINE // 4)
 
         for t in range(PACK):
             nc.scalar.activation(out=ya_win[t][:, S:], in_=db_banks[t][:], func=ACT.Abs)
         for t in range(PACK):
             nc.scalar.activation(out=db_win[t][:, :S], in_=ya_win[t][:, S:], func=ACT.Ln, bias=half_col[:])
 
-        y_diff = planes("y_diff")
+        factor = row_tiles("factor", S)
         for t in range(PACK):
-            nc.vector.tensor_tensor(y_diff[t][:], ya_win[t][:].indirect(n1_l[:]), own[t], ALU.subtract)
+            nc.vector.tensor_tensor(factor[t][:], ya_win[t][:].indirect(n1_l[:]), own[t], ALU.subtract)
 
-        w3_grouped = round_weight("w3", w3_raw, (nc.vector.tensor_copy, nc.vector.tensor_copy))
+        w3_grouped = reuse.tile([P, PACK, P, PACK], BF16, name="w3_grouped", offset=5 * S, align_bytes=64)
+        round_weight(w3_grouped, w3_raw, (nc.vector.tensor_copy, nc.vector.tensor_copy))
         w3_mx = quantize_weight("w3", w3_grouped)
 
         z_rows = pool.tile([P, PACK, S], F32, name="z_rows")
         for t in range(PACK):
-            nc.scalar.activation(out=y_diff[t][:], in_=y_diff[t][:], func=ACT.Tanh, scale=gn_inv[:, t : t + 1])
-            if t < 4:
-                nc.vector.tensor_tensor(z_rows[:, t, :], ya_win[t][:].indirect(n2_l[:]), y_diff[t][:], ALU.mult)
-        for t in range(4, PACK):
-            y_far = pool.tile([P, S], F32, name="y_far", tag="after_tanh")
-            nc.scalar.activation(out=y_far[:], in_=ya_win[t][:].indirect(n2_l[:]), func=ACT.Copy)
-            nc.vector.tensor_tensor(z_rows[:, t, :], y_far[:], y_diff[t][:], ALU.mult)
+            nc.scalar.activation(out=factor[t][:], in_=factor[t][:], func=ACT.Tanh, scale=gn_inv[:, t : t + 1])
+            nc.vector.tensor_tensor(z_rows[:, t, :], ya_win[t][:].indirect(n2_l[:]), factor[t][:], ALU.mult)
 
         z_grouped = pool.tile([P, S, PACK], BF16, name="z_grouped", align_bytes=64)
         z_mx = mx_tiles("z")
-        for h in range(2):
-            quantize_half(z_rows, z_grouped, z_mx, h, (nc.vector.tensor_copy, nc.vector.tensor_copy)[h])
-            product(ya_banks, w3_mx, z_mx, cols(h))
+        for part in halves:
+            quantize_rows(z_rows, z_grouped, z_mx, part)
+            product(ya_banks, w3_mx, z_mx, part)
 
-        inv_den = y_diff
         z2_rows = pool.tile([P, PACK, S], F32, name="z2_rows")
         for t in range(PACK):
-            nc.scalar.activation(out=inv_den[t][:], in_=db_win[t][:].indirect(n3_l[:]), func=ACT.Exp, scale=-1.0)
+            nc.scalar.activation(out=factor[t][:], in_=db_win[t][:].indirect(n3_l[:]), func=ACT.Exp, scale=-1.0)
             nc.vector.scalar_tensor_tensor(
-                z2_rows[:, t, :], db_banks[t][:], gs_c[:, t : t + 1], inv_den[t][:], ALU.mult, ALU.mult
+                z2_rows[:, t, :], db_banks[t][:], gs_c[:, t : t + 1], factor[t][:], ALU.mult, ALU.mult
             )
 
         for t in range(PACK):
             nc.scalar.copy(out=ya_win[t][:, :S], in_=ya_banks[t][:])
-            if "V" in (U4[t], U5[t]):
+            if t == 0:
+                nc.vector.tensor_copy(own[t], ya_win[t][:, :S])
+            elif t < max(N4_TILES_ON_VECTOR, N5_TILES_ON_VECTOR):
                 nc.sync.dma_start(own[t], ya_win[t][:, :S])
 
         z2_grouped = pool.tile([P, S, PACK], BF16, name="z2_grouped", align_bytes=64)
         z2_mx = mx_tiles("z2")
-        for h in range(2):
-            quantize_half(z2_rows, z2_grouped, z2_mx, h, (nc.vector.tensor_copy, nc.vector.tensor_copy)[h])
-            product(db_banks, x_cand, z2_mx, cols(h))
+        for part in halves:
+            quantize_rows(z2_rows, z2_grouped, z2_mx, part)
+            product(db_banks, (cand_codes, cand_scales), z2_mx, part)
 
-        first = planes("first")
-        second = planes("second")
-        b_far = planes("b_far")
-        out_rows = out.rearrange("(p t) s -> p t s", t=PACK)
-
-        def diff(dst, lst, who, t):
-            if who == "S":
+        def looked_up_less_own(dst, lst, t, on_vector):
+            if on_vector:
+                nc.vector.tensor_tensor(dst[:], ya_win[t][:].indirect(lst[:]), own[t], ALU.subtract)
+            else:
                 nc.scalar.activation(out=dst[:], in_=ya_win[t][:].indirect(lst[:]), func=ACT.Copy)
                 nc.vector.tensor_tensor(dst[:], dst[:], ya_banks[t][:], ALU.subtract)
-            else:
-                nc.vector.tensor_tensor(dst[:], ya_win[t][:].indirect(lst[:]), own[t], ALU.subtract)
 
+        term4 = row_tiles("term4", S)
+        diff5 = row_tiles("diff5", S)
+        term5 = row_tiles("term5", S)
+        out_rows = out.rearrange("(p t) s -> p t s", t=PACK)
         for t in range(PACK):
-            diff(first[t], n4_l, U4[t], t)
-            diff(second[t], n5_l, U5[t], t)
-            nc.scalar.activation(out=db_win[t][:, :S], in_=db_banks[t][:], func=ACT.Copy, scale=0.03125)
-            nc.vector.scalar_tensor_tensor(first[t][:], db_banks[t][:], 0.0625, first[t][:], ALU.mult, ALU.mult)
-            if B6[t] == "S":
-                nc.scalar.activation(out=b_far[t][:], in_=db_win[t][:].indirect(n6_l[:]), func=ACT.Copy)
-            else:
-                nc.vector.tensor_tensor(b_far[t][:], db_win[t][:].indirect(n6_l[:]), second[t][:], ALU.mult)
-            for part in (cols(0), cols(1)) if t == PACK - 1 else (whole,):
-                if B6[t] == "S":
-                    nc.vector.tensor_tensor(b_far[t][:, part], second[t][:, part], b_far[t][:, part], ALU.mult)
-            for part in (cols(0), cols(1)) if t == PACK - 1 else (whole,):
-                nc.vector.tensor_tensor(first[t][:, part], first[t][:, part], b_far[t][:, part], ALU.add)
-                nc.sync.dma_start(out_rows[:, t, part], first[t][:, part])
+            looked_up_less_own(term4[t], n4_l, t, t < N4_TILES_ON_VECTOR)
+            looked_up_less_own(diff5[t], n5_l, t, t < N5_TILES_ON_VECTOR)
+            nc.scalar.activation(out=db_win[t][:, :S], in_=db_banks[t][:], func=ACT.Copy, scale=0.5 / 16)
+            nc.vector.scalar_tensor_tensor(term4[t][:], db_banks[t][:], 1 / 16, term4[t][:], ALU.mult, ALU.mult)
+            parts = halves if t == PACK - 1 else (whole,)
+            for part in parts:
+                entries = n6_l[:, part.start // PER_COLUMN : part.stop // PER_COLUMN]
+                nc.scalar.activation(out=term5[t][:, part], in_=db_win[t][:].indirect(entries), func=ACT.Copy)
+            for part in parts:
+                nc.vector.tensor_tensor(term5[t][:, part], diff5[t][:, part], term5[t][:, part], ALU.mult)
+            for part in parts:
+                nc.vector.tensor_tensor(term4[t][:, part], term4[t][:, part], term5[t][:, part], ALU.add)
+                nc.sync.dma_start(out_rows[:, t, part], term4[t][:, part])

from contextlib import ExitStack

import concourse.mybir as mybir

F32 = mybir.dt.float32
BF16 = mybir.dt.bfloat16
I32 = mybir.dt.int32
U32 = mybir.dt.uint32
U16 = mybir.dt.uint16
U8 = mybir.dt.uint8
FP8X4 = mybir.dt.float8_e4m3fn_x4
ACT = mybir.ActivationFunctionType
ALU = mybir.AluOpType

P = 128
PACK = 4
T = 2048
S = 512
HALF = S // 2
PER_COLUMN = 16
LINE = 16
TINY_GAIN = 2.0**-120
N4_TILES_ON_VECTOR = 2
N5_TILES_ON_VECTOR = 1
FLOPS = 4 * 2 * S * S * S


def tile_picked_tfcdflowbfdifnorm_none_p_kernel(
    tc, x_words, x_scales, w1, w2, gn, w3, gs, offs, two, n1, n2, n3, cand, n4, n5, n6, out
):
    nc = tc.nc
    with ExitStack() as ctx:
        pool = ctx.enter_context(tc.tile_pool(name="held", bufs=1))
        reuse = ctx.enter_context(tc.tile_pool(name="reuse", bufs=1))
        psum = ctx.enter_context(tc.psum_pool(name="psum", bufs=1))

        halves = (slice(0, HALF), slice(HALF, S))
        whole = slice(0, S)

        def load_list(name, src):
            lst = pool.tile([P, S // PER_COLUMN], U16, name=name)
            nc.sync.dma_start(lst[:], src)
            return lst

        def load_weight(name, w):
            raws = []
            for h, part in enumerate(halves):
                raw = pool.tile([P, PACK, HALF], F32, name=f"{name}_raw{h}")
                nc.sync.dma_start(raw[:], w.rearrange("(p j) c -> p j c", j=PACK)[:, :, part])
                raws.append(raw)
            return raws

        def load_gain(name, gain):
            col = pool.tile([P, PACK], F32, name=name)
            nc.sync.dma_start(col[:], gain.rearrange("(p t) o -> p (t o)", t=PACK))
            return col

        def row_tiles(name, width):
            return [pool.tile([P, width], F32, name=f"{name}{t}") for t in range(PACK)]

        def mx_tiles(name):
            codes = pool.tile([P, S], U32, name=f"{name}_codes", align_bytes=64)
            scales = pool.tile([P, S], U8, name=f"{name}_scales", align_bytes=64)
            return codes, scales

        def round_weight(grouped, raws, copies):
            m_half = HALF // PACK
            for h in range(2):
                copies[h](
                    out=grouped[:, :, h * m_half : (h + 1) * m_half, :].rearrange("p t m j -> p m t j"),
                    in_=raws[h][:].rearrange("p j (m t) -> p m t j", t=PACK),
                )

        def quantize_weight(name, grouped):
            codes, scales = mx_tiles(name)
            nc.vector.quantize_mx(
                out=codes[:].bitcast(FP8X4), scales=scales[:], in_=grouped[:].rearrange("p t m j -> p (t m j)")
            )
            return codes, scales

        def deal(dst, src, run):
            nc.vector.tensor_copy(
                dst[:].rearrange("p (t g r) -> p g t r", t=PACK, r=run),
                src[:].rearrange("p (g r t) -> p g t r", t=PACK, r=run),
            )

        def product(banks, stationary, moving, n_cols):
            for t in range(PACK):
                m_cols = slice(t * P, (t + 1) * P)
                nc.tensor.matmul_mx(
                    out=banks[t][:, n_cols],
                    lhsT=stationary[0][:, m_cols].bitcast(FP8X4),
                    lhsT_scale=stationary[1][:, m_cols],
                    rhs=moving[0][:, n_cols].bitcast(FP8X4),
                    rhs_scale=moving[1][:, n_cols],
                    start=True,
                    stop=True,
                )

        def quantize_rows(rows, grouped, mx, part):
            nc.vector.tensor_copy(
                out=grouped[:, part, :].rearrange("p (c i) t -> p c t i", i=4),
                in_=rows[:, :, part].rearrange("p t (c i) -> p c t i", i=4),
            )
            nc.vector.quantize_mx(
                out=mx[0][:, part].bitcast(FP8X4),
                scales=mx[1][:, part],
                in_=grouped[:, part, :].rearrange("p s t -> p (s t)"),
            )

        table_scales = pool.tile([P, T], U8, name="table_scales")
        nc.gpsimd.memset(table_scales[:].bitcast(I32), 0)
        half_col = pool.tile([P, 1], F32, name="half_col")
        nc.gpsimd.memset(half_col[:], 0.5)

        warm = pool.tile([P, 1], F32, name="warm")
        nc.scalar.activation(out=warm[:], in_=half_col[:], func=ACT.Ln)

        offs_l = load_list("offs_l", offs)
        for q in range(4):
            nc.sync.dma_start(
                table_scales[32 * q : 32 * q + 4, :].bitcast(I32), x_scales[0, 4 * q : 4 * q + 4, :].bitcast(I32)
            )
        two_l = load_list("two_l", two)
        w1_raw = load_weight("w1", w1)
        cand_l = load_list("cand_l", cand)
        table_words = pool.tile([P, T], U32, name="table_words")
        nc.sync.dma_start(table_words[:].bitcast(I32), x_words[0].rearrange("p n r -> p (n r)").bitcast(I32))
        w2_raw = load_weight("w2", w2)
        gn_c = load_gain("gn_c", gn)
        n1_l = load_list("n1_l", n1)
        w3_raw = load_weight("w3", w3)
        n2_l = load_list("n2_l", n2)
        n3_l = load_list("n3_l", n3)
        gs_c = load_gain("gs_c", gs)
        n4_l = load_list("n4_l", n4)
        n5_l = load_list("n5_l", n5)
        n6_l = load_list("n6_l", n6)

        ya_banks = [psum.tile([P, S], F32, name=f"ya_bank{t}") for t in range(PACK)]
        db_banks = [psum.tile([P, S], F32, name=f"db_bank{t}") for t in range(PACK)]

        x_offs = mx_tiles("x_offs")
        x_two = mx_tiles("x_two")
        nc.vector.tensor_copy(x_offs[1][:], table_scales[:].indirect(offs_l[:]))
        nc.vector.tensor_copy(x_two[1][:], table_scales[:].indirect(two_l[:]))
        listed_scales = pool.tile([P, S], U8, name="listed_scales", align_bytes=64)
        nc.vector.tensor_copy(listed_scales[:], table_scales[:].indirect(cand_l[:]))
        w1_grouped = pool.tile([P, PACK, P, PACK], BF16, name="w1_grouped", align_bytes=64)
        round_weight(w1_grouped, w1_raw, (nc.scalar.copy, nc.scalar.copy))
        w1_mx = quantize_weight("w1", w1_grouped)
        nc.vector.tensor_copy(x_offs[0][:], table_words[:].indirect(offs_l[:]))
        product(ya_banks, w1_mx, x_offs, whole)
        nc.vector.tensor_copy(x_two[0][:], table_words[:].indirect(two_l[:]))

        w2_grouped = reuse.tile([P, PACK, P, PACK], BF16, name="w2_grouped", offset=0, align_bytes=64)
        round_weight(w2_grouped, w2_raw, (nc.scalar.copy, nc.vector.tensor_copy))

        ya_win = row_tiles("ya_win", 2 * S)
        db_win = row_tiles("db_win", 2 * S)
        own = [db_win[t][:, S:] for t in range(PACK)]

        gn_inv = pool.tile([P, PACK], F32, name="gn_inv")
        nc.vector.scalar_tensor_tensor(gn_inv[:], gn_c[:], -1.0, gn_c[:], ALU.mult, ALU.max)
        nc.vector.scalar_tensor_tensor(gn_inv[:], gn_inv[:], TINY_GAIN, gn_c[:], ALU.is_lt, ALU.add)
        nc.vector.reciprocal(gn_inv[:], gn_inv[:])
        for t in range(PACK):
            nc.scalar.activation(out=ya_win[t][:, :S], in_=ya_banks[t][:], func=ACT.Copy, scale=gn_c[:, t : t + 1])
            nc.sync.dma_start(own[t], ya_win[t][:, :S])

        w2_mx = quantize_weight("w2", w2_grouped)
        product(db_banks, w2_mx, x_two, whole)

        listed_codes = reuse.tile([P, S], U32, name="listed_codes", offset=0, align_bytes=64)
        nc.vector.tensor_copy(listed_codes[:], table_words[:].indirect(cand_l[:]))
        cand_codes = pool.tile([P, S], U32, name="cand_codes", align_bytes=64)
        cand_scales = reuse.tile([P, S], U8, name="cand_scales", offset=4 * S, align_bytes=64)
        deal(cand_scales, listed_scales, LINE)
        deal(cand_codes, listed_codes, LINE // 4)

        for t in range(PACK):
            nc.scalar.activation(out=ya_win[t][:, S:], in_=db_banks[t][:], func=ACT.Abs)
        for t in range(PACK):
            nc.scalar.activation(out=db_win[t][:, :S], in_=ya_win[t][:, S:], func=ACT.Ln, bias=half_col[:])

        factor = row_tiles("factor", S)
        for t in range(PACK):
            nc.vector.tensor_tensor(factor[t][:], ya_win[t][:].indirect(n1_l[:]), own[t], ALU.subtract)

        w3_grouped = reuse.tile([P, PACK, P, PACK], BF16, name="w3_grouped", offset=5 * S, align_bytes=64)
        round_weight(w3_grouped, w3_raw, (nc.vector.tensor_copy, nc.vector.tensor_copy))
        w3_mx = quantize_weight("w3", w3_grouped)

        z_rows = pool.tile([P, PACK, S], F32, name="z_rows")
        for t in range(PACK):
            nc.scalar.activation(out=factor[t][:], in_=factor[t][:], func=ACT.Tanh, scale=gn_inv[:, t : t + 1])
            nc.vector.tensor_tensor(z_rows[:, t, :], ya_win[t][:].indirect(n2_l[:]), factor[t][:], ALU.mult)

        z_grouped = pool.tile([P, S, PACK], BF16, name="z_grouped", align_bytes=64)
        z_mx = mx_tiles("z")
        for part in halves:
            quantize_rows(z_rows, z_grouped, z_mx, part)
            product(ya_banks, w3_mx, z_mx, part)

        z2_rows = pool.tile([P, PACK, S], F32, name="z2_rows")
        for t in range(PACK):
            nc.scalar.activation(out=factor[t][:], in_=db_win[t][:].indirect(n3_l[:]), func=ACT.Exp, scale=-1.0)
            nc.vector.scalar_tensor_tensor(
                z2_rows[:, t, :], db_banks[t][:], gs_c[:, t : t + 1], factor[t][:], ALU.mult, ALU.mult
            )

        for t in range(PACK):
            nc.scalar.copy(out=ya_win[t][:, :S], in_=ya_banks[t][:])
            if t == 0:
                nc.vector.tensor_copy(own[t], ya_win[t][:, :S])
            elif t < max(N4_TILES_ON_VECTOR, N5_TILES_ON_VECTOR):
                nc.sync.dma_start(own[t], ya_win[t][:, :S])

        z2_grouped = pool.tile([P, S, PACK], BF16, name="z2_grouped", align_bytes=64)
        z2_mx = mx_tiles("z2")
        for part in halves:
            quantize_rows(z2_rows, z2_grouped, z2_mx, part)
            product(db_banks, (cand_codes, cand_scales), z2_mx, part)

        def looked_up_less_own(dst, lst, t, on_vector):
            if on_vector:
                nc.vector.tensor_tensor(dst[:], ya_win[t][:].indirect(lst[:]), own[t], ALU.subtract)
            else:
                nc.scalar.activation(out=dst[:], in_=ya_win[t][:].indirect(lst[:]), func=ACT.Copy)
                nc.vector.tensor_tensor(dst[:], dst[:], ya_banks[t][:], ALU.subtract)

        term4 = row_tiles("term4", S)
        diff5 = row_tiles("diff5", S)
        term5 = row_tiles("term5", S)
        out_rows = out.rearrange("(p t) s -> p t s", t=PACK)
        for t in range(PACK):
            looked_up_less_own(term4[t], n4_l, t, t < N4_TILES_ON_VECTOR)
            looked_up_less_own(diff5[t], n5_l, t, t < N5_TILES_ON_VECTOR)
            nc.scalar.activation(out=db_win[t][:, :S], in_=db_banks[t][:], func=ACT.Copy, scale=0.5 / 16)
            nc.vector.scalar_tensor_tensor(term4[t][:], db_banks[t][:], 1 / 16, term4[t][:], ALU.mult, ALU.mult)
            parts = halves if t == PACK - 1 else (whole,)
            for part in parts:
                entries = n6_l[:, part.start // PER_COLUMN : part.stop // PER_COLUMN]
                nc.scalar.activation(out=term5[t][:, part], in_=db_win[t][:].indirect(entries), func=ACT.Copy)
            for part in parts:
                nc.vector.tensor_tensor(term5[t][:, part], diff5[t][:, part], term5[t][:, part], ALU.mult)
            for part in parts:
                nc.vector.tensor_tensor(term4[t][:, part], term4[t][:, part], term5[t][:, part], ALU.add)
                nc.sync.dma_start(out_rows[:, t, part], term4[t][:, part])
